import numpy as np
import ml_dtypes


def mxq(x, axis, fmt="e4m3"):
    dtype, down = {"e4m3": (ml_dtypes.float8_e4m3fn, 7), "e5m2": (ml_dtypes.float8_e5m2, 14)}[fmt]
    v = np.moveaxis(np.asarray(x, np.float32).astype(ml_dtypes.bfloat16).astype(np.float64), axis, -1)
    blocks = v.reshape(v.shape[:-1] + (-1, 32))
    amax = np.abs(blocks).max(-1, keepdims=True)
    byte = np.maximum(np.where(amax > 0, np.frexp(amax)[1] - 1 + 127, 0) - down, 1)
    scale = np.exp2(byte - 127.0)
    codes = (blocks / scale).astype(np.float32).astype(dtype).astype(np.float64)
    return np.moveaxis((codes * scale).reshape(v.shape), -1, axis)


WIDE = False


def mx_kscale(k):
    if not WIDE:
        return np.ones(k)
    levels = np.array([10, -10, 5, -5, 0])
    if k % 512:
        return np.exp2(np.random.permutation(np.resize(levels, k // 32))).repeat(32)
    a = np.empty((k // 512, 16))
    for p in range(k // 512):
        a[p, :8] = np.random.permutation(np.resize(levels, 8))
        for g in range(8):
            far = levels[np.abs(levels - a[p, g]) >= 10]
            a[p, g + 8] = far[np.random.randint(len(far))]
    return np.exp2(a.ravel()).repeat(32)


BF16 = ml_dtypes.bfloat16


def bf(x):
    return np.asarray(x, np.float32).astype(BF16)


def f64(x):
    return np.asarray(x).astype(np.float64)


E2M1 = np.array([0.0, 0.5, 1.0, 1.5, 2.0, 3.0, 4.0, 6.0, -0.0, -0.5, -1.0, -1.5, -2.0, -3.0, -4.0, -6.0])


def pack_weight(w, fmt):
    k, n = w.shape
    w = f64(bf(w)).reshape(k // 32, 32, n)
    amax = np.abs(w).max(1)
    if fmt == "e4m3":
        byte = np.frexp(amax)[1] - 1 + 127 - 7
    else:
        mant, ex = np.frexp(amax / 6.0)
        byte = np.where(mant > 0.5, ex, ex - 1) + 127
    byte = np.clip(np.where(amax > 0, byte, 1), 1, 254)
    scaled = (w * np.exp2(127.0 - byte)[:, None, :]).reshape(k, n).astype(np.float32)
    by_word = np.ascontiguousarray(scaled.reshape(k // 512, 128, 4, n).transpose(0, 1, 3, 2))
    if fmt == "e4m3":
        words = by_word.astype(ml_dtypes.float8_e4m3fn).view(np.uint8)
    else:
        c = by_word.astype(ml_dtypes.float4_e2m1fn).view(np.uint8) & 0xF
        words = c[..., 0::2] | (c[..., 1::2] << 4)
    return np.ascontiguousarray(words), np.ascontiguousarray(byte.astype(np.uint8).reshape(k // 512, 16, n))


def unpack_weight(words, scales, fmt):
    g, p, n, _ = words.shape
    if fmt == "e4m3":
        vals = np.ascontiguousarray(words).view(ml_dtypes.float8_e4m3fn).astype(np.float64)
    else:
        nib = np.empty((g, p, n, 4), np.uint8)
        nib[..., 0::2] = words & 0xF
        nib[..., 1::2] = words >> 4
        vals = E2M1[nib]
    vals = vals * np.repeat(np.exp2(scales.astype(np.float64) - 127.0), 8, axis=1)[..., None]
    return vals.transpose(0, 1, 3, 2).reshape(g * 512, n)
def pack4(w):
    words, scales = pack_weight(w, "e2m1")
    return words.reshape(words.shape[0], 128, -1), scales


def unpack4(words, scales):
    return unpack_weight(words.reshape(words.shape[0], 128, -1, 2), scales, "e2m1")


M, K, N, V = 1024, 2048, 1024, 2048


def setup_inputs():
    s = mx_kscale(K)
    t = mx_kscale(N)
    x = np.random.standard_normal((K, M)) * s[:, None]
    w = np.random.standard_normal((K, N)) / np.sqrt(K) / s[:, None]
    u = 1.5 * np.random.standard_normal((N, V)) / np.sqrt(N) / t[:, None]
    x_words, x_scales = pack4(x)
    w_words, w_scales = pack4(w)
    u_words, u_scales = pack_weight(u, "e4m3")
    return {"x_words": x_words, "x_scales": x_scales,
            "w_words": w_words, "w_scales": w_scales,
            "gain": bf((1 + 0.1 * np.random.standard_normal(N)) * t),
            "u_words": u_words, "u_scales": u_scales,
            "bias": bf(0.3 * np.random.standard_normal(V)),
            "prior_ratio": bf(np.exp(0.5 * np.random.standard_normal(V)))}


def reference(x_words, x_scales, w_words, w_scales, gain, u_words, u_scales, bias, prior_ratio):
    x = unpack4(x_words, x_scales)
    w = unpack4(w_words, w_scales)
    u = unpack_weight(u_words, u_scales, "e4m3")
    z = x.T @ w
    h = np.tanh(z) * f64(gain)
    logits = mxq(h, 1, "e4m3") @ u
    return logits + f64(bias) - np.log(f64(prior_ratio))

@@ -1,0 +1,212 @@
+from contextlib import ExitStack
+
+import concourse.mybir as mybir
+
+M, K, N, V = 1024, 2048, 1024, 2048
+FLOPS = 2 * M * K * N + 2 * M * N * V
+BYTES = 2 * (K * M // 2 + K // 32 * M) + N * V + N // 32 * V + 2 * N + 4 * V + 4 * M * V
+
+F32 = mybir.dt.float32
+BF16 = mybir.dt.bfloat16
+I32 = mybir.dt.int32
+U32 = mybir.dt.uint32
+U8 = mybir.dt.uint8
+FP4X4 = mybir.dt.float4_e2m1fn_x4
+FP8X4 = mybir.dt.float8_e4m3fn_x4
+ADD = mybir.AluOpType.add
+SUB = mybir.AluOpType.subtract
+MULT = mybir.AluOpType.mult
+LN = mybir.ActivationFunctionType.Ln
+TANH = mybir.ActivationFunctionType.Tanh
+
+P = 128
+KG = K // 512
+NG = N // 512
+HALF = 512
+Q = 256
+
+
+def tile_ctc_prior_head_s4_kernel(
+    tc, x_words, x_scales, w_words, w_scales, gain, u_words, u_scales, bias, prior_ratio, out
+):
+    nc = tc.nc
+    with ExitStack() as ctx:
+        keep = ctx.enter_context(tc.tile_pool(name="keep", bufs=1))
+        th_pool = ctx.enter_context(tc.tile_pool(name="th", bufs=3))
+        hb_pool = ctx.enter_context(tc.tile_pool(name="hb", bufs=3))
+        res_pool = ctx.enter_context(tc.tile_pool(name="res", bufs=6))
+        psum = ctx.enter_context(tc.psum_pool(name="psum", bufs=1))
+        ctx.enter_context(tc.manual_schedule())
+
+        x_w = [keep.tile([P, 2 * M], U8, name=f"x_w{g}", align_bytes=64) for g in range(KG)]
+        w_raw = [keep.tile([P, 2 * N], U8, name=f"w_raw{g}", align_bytes=64) for g in range(KG)]
+        x_s = keep.tile([P, KG, M], U8, name="x_s", align_bytes=64)
+        ws_raw = keep.tile([P, KG, N], U8, name="ws_raw", align_bytes=64)
+        u_s = keep.tile([P, NG, V], U8, name="u_s", align_bytes=64)
+        u_w = [keep.tile([P, V], U32, name=f"u_w{g}", align_bytes=64) for g in range(NG)]
+        w_p = [[keep.tile([P, 4, P, 2], U8, name=f"w_p{c}_{g}", align_bytes=64) for g in range(KG)] for c in range(NG)]
+        ws_p = [[keep.tile([P, 4, P], U8, name=f"ws_p{c}_{g}", align_bytes=64) for g in range(KG)] for c in range(NG)]
+        gain_c = keep.tile([P, NG, 4], BF16, name="gain_c")
+        prior_b = keep.tile([P, V], BF16, name="prior_b")
+        bias_b = keep.tile([P, V], BF16, name="bias_b")
+        log_p = keep.tile([P, V], F32, name="log_p")
+        shift = keep.tile([P, V], F32, name="shift")
+        warm = keep.tile([P, 2], F32, name="warm")
+        h_c = [[keep.tile([P, Q], U32, name=f"h_c{c}_{q}", align_bytes=64) for q in range(4)] for c in range(NG)]
+        h_s = [[keep.tile([P, Q], U8, name=f"h_s{c}_{q}", align_bytes=64) for q in range(4)] for c in range(NG)]
+
+        def load_words(engine, tile, words, g):
+            engine.dma_start(out=tile[:].bitcast(I32), in_=words[g].bitcast(I32))
+
+        def load_scale_quad(engine, tile, scales, quad):
+            engine.dma_start(
+                out=tile[32 * quad : 32 * quad + 4].bitcast(I32),
+                in_=scales[:, 4 * quad : 4 * quad + 4, :].rearrange("g q n -> q g n").bitcast(I32),
+            )
+
+        load_words(nc.sync, w_raw[0], w_words, 0)
+        load_words(nc.gpsimd, x_w[0], x_words, 0)
+        nc.vector.memset(ws_raw[:].bitcast(I32), 0)
+        nc.vector.memset(x_s[:].bitcast(I32), 0)
+        nc.vector.memset(warm[:], 1.0)
+        nc.scalar.activation(out=warm[:, 1:2], in_=warm[:, 0:1], func=LN)
+        for quad in range(4):
+            load_scale_quad(nc.sync, ws_raw, w_scales, quad)
+        for quad in range(4):
+            load_scale_quad(nc.sync if quad < 3 else nc.gpsimd, x_s, x_scales, quad)
+        nc.gpsimd.dma_start(out=gain_c[:], in_=gain.rearrange("(c p t) -> p c t", c=NG, t=4))
+        for g in (1, 2):
+            load_words(nc.sync, w_raw[g], w_words, g)
+            load_words(nc.sync, x_w[g], x_words, g)
+        nc.sync.dma_start(out=prior_b[:], in_=prior_ratio.partition_broadcast(P))
+        load_words(nc.sync, w_raw[3], w_words, 3)
+        load_words(nc.sync, x_w[3], x_words, 3)
+        nc.sync.dma_start(out=bias_b[:], in_=bias.partition_broadcast(P))
+        nc.vector.memset(u_s[:].bitcast(I32), 0)
+        for quad in range(4):
+            load_scale_quad(nc.sync, u_s, u_scales, quad)
+        for c in range(NG):
+            nc.sync.dma_start(out=u_w[c][:].bitcast(I32), in_=u_words[c].rearrange("p n t -> p (n t)").bitcast(I32))
+
+        def order_scales(c, g):
+            nc.vector.tensor_copy(
+                out=ws_p[c][g][:],
+                in_=ws_raw[:, g, 512 * c : 512 * (c + 1)].rearrange("p (m t) -> p t m", t=4),
+            )
+
+        def order_words(c, g):
+            nc.vector.tensor_copy(
+                out=w_p[c][g][:],
+                in_=w_raw[g][:, 1024 * c : 1024 * (c + 1)].rearrange("p (m t e) -> p t m e", t=4, e=2),
+            )
+
+        for c, g in ((0, 0), (0, 1), (1, 0), (0, 2), (1, 1), (0, 3), (1, 2), (1, 3)):
+            order_scales(c, g)
+            order_words(c, g)
+        nc.scalar.activation(out=log_p[:], in_=prior_b[:], func=LN)
+        nc.scalar.activation(out=warm[:, 1:2], in_=warm[:, 0:1], func=TANH)
+        nc.vector.tensor_tensor(out=shift[:], in0=bias_b[:], in1=log_p[:], op=SUB)
+
+        def bank_tile(i):
+            return psum.tile([P, 512], F32, name=f"bank{i}", tag=f"bank{i}")
+
+        def project(dst, c, g, t, m0, width):
+            nc.tensor.matmul_mx(
+                out=dst,
+                lhsT=w_p[c][g][:, t].rearrange("p m e -> p (m e)").bitcast(FP4X4),
+                lhsT_scale=ws_p[c][g][:, t],
+                rhs=x_w[g][:, 2 * m0 : 2 * (m0 + width)].bitcast(FP4X4),
+                rhs_scale=x_s[:, g, m0 : m0 + width],
+                start=(g == 0),
+                stop=(g == KG - 1),
+            )
+
+        def multiply(c, q, th, n0):
+            hb = hb_pool.tile([P, Q, 4], BF16, name="hb", align_bytes=64)
+            nc.vector.tensor_tensor(
+                out=hb[:].rearrange("p (b i) t -> p b t i", i=4),
+                in0=th[:, :, n0 : n0 + Q].rearrange("p t (b i) -> p b t i", i=4),
+                in1=gain_c[:, c, :].unsqueeze(1).unsqueeze(3).to_broadcast([P, Q // 4, 4, 4]),
+                op=MULT,
+            )
+            return hb
+
+        def quantise(c, q, hb):
+            nc.vector.quantize_mx(
+                out=h_c[c][q][:].bitcast(FP8X4), scales=h_s[c][q][:], in_=hb[:].rearrange("p n t -> p (n t)")
+            )
+
+        banks = [[bank_tile(4 * h + t) for t in range(4)] for h in range(2)]
+        for g in range(KG):
+            for h in range(2):
+                for t in range(4):
+                    project(banks[h][t][:], 0, g, t, HALF * h, HALF)
+        th0 = [keep.tile([P, 4, HALF], F32, name=f"th0_{h}") for h in range(2)]
+        for h in range(2):
+            for t in range(4):
+                nc.scalar.activation(out=th0[h][:, t, :], in_=banks[h][t][:], func=TANH)
+
+        def project_quarter(q):
+            th = th_pool.tile([P, 4, Q], F32, name="th")
+            for pair in range(2):
+                bank = bank_tile(2 * (q % 2) + pair)
+                for j in range(2):
+                    for g in range(KG):
+                        project(bank[:, Q * j : Q * (j + 1)], 1, g, 2 * pair + j, Q * q, Q)
+                nc.scalar.activation(
+                    out=th[:, 2 * pair : 2 * pair + 2, :].rearrange("p t n -> p (t n)"), in_=bank[:], func=TANH
+                )
+            return th
+
+        def score(q, side, off):
+            step = 0
+            for m in range(2):
+                for v in range(4):
+                    bank = bank_tile(4 + step % 4 if q < 2 else (4 + step) % 8)
+                    for c in range(NG):
+                        nc.tensor.matmul_mx(
+                            out=bank[:],
+                            lhsT=h_c[c][q][:, P * m : P * (m + 1)].bitcast(FP8X4),
+                            lhsT_scale=h_s[c][q][:, P * m : P * (m + 1)],
+                            rhs=u_w[c][:, 512 * v : 512 * (v + 1)].bitcast(FP8X4),
+                            rhs_scale=u_s[:, c, 512 * v : 512 * (v + 1)],
+                            start=(c == 0),
+                            stop=(c == NG - 1),
+                        )
+                    res = res_pool.tile([P, 512], F32, name="res")
+                    if step in off:
+                        raw = res_pool.tile([P, 512], F32, name="raw")
+                        nc.scalar.copy(out=raw[:], in_=bank[:])
+                        nc.gpsimd.tensor_tensor(out=res[:], in0=raw[:], in1=shift[:, 512 * v : 512 * (v + 1)], op=ADD)
+                    else:
+                        nc.vector.tensor_tensor(out=res[:], in0=bank[:], in1=shift[:, 512 * v : 512 * (v + 1)], op=ADD)
+                    m0 = Q * q + P * m
+                    nc.sync.dma_start(out=out[m0 : m0 + P, 512 * v : 512 * (v + 1)], in_=res[:])
+                    for job in side.get(step, []):
+                        job()
+                    step += 1
+
+        held = {}
+
+        def mul_job(c, q, th, n0):
+            held[(c, q)] = multiply(c, q, th, n0)
+
+        def quant_job(c, q):
+            quantise(c, q, held[(c, q)])
+
+        mul_job(0, 0, th0[0], 0)
+        mul_job(0, 1, th0[0], Q)
+        quant_job(0, 0)
+        th_q0 = project_quarter(0)
+        th_q1 = project_quarter(1)
+        mul_job(1, 0, th_q0, 0)
+        quant_job(0, 1)
+        quant_job(1, 0)
+        mul_job(0, 2, th0[1], 0)
+        score(0, {1: [lambda: mul_job(1, 1, th_q1, 0)], 2: [lambda: quant_job(0, 2)], 3: [lambda: quant_job(1, 1)]}, (1, 3, 5))
+        th_q2 = project_quarter(2)
+        mul_job(0, 3, th0[1], Q)
+        score(1, {1: [lambda: mul_job(1, 2, th_q2, 0)], 2: [lambda: quant_job(0, 3)], 3: [lambda: quant_job(1, 2)]}, (1, 3, 5))
+        th_q3 = project_quarter(3)
+        score(2, {1: [lambda: mul_job(1, 3, th_q3, 0)], 3: [lambda: quant_job(1, 3)]}, (1, 3, 5))
+        score(3, {}, (0, 2, 4, 6))

@@ -16,6 +16,7 @@ FP8X4 = mybir.dt.float8_e4m3fn_x4
 ADD = mybir.AluOpType.add
 SUB = mybir.AluOpType.subtract
 MULT = mybir.AluOpType.mult
+COPY = mybir.ActivationFunctionType.Copy
 LN = mybir.ActivationFunctionType.Ln
 TANH = mybir.ActivationFunctionType.Tanh
 
@@ -33,8 +34,9 @@ def tile_ctc_prior_head_s4_kernel(
     with ExitStack() as ctx:
         keep = ctx.enter_context(tc.tile_pool(name="keep", bufs=1))
         th_pool = ctx.enter_context(tc.tile_pool(name="th", bufs=3))
-        hb_pool = ctx.enter_context(tc.tile_pool(name="hb", bufs=3))
-        res_pool = ctx.enter_context(tc.tile_pool(name="res", bufs=6))
+        hb_pool = ctx.enter_context(tc.tile_pool(name="hb", bufs=4))
+        res_pool = ctx.enter_context(tc.tile_pool(name="res", bufs=10))
+        raw_pool = ctx.enter_context(tc.tile_pool(name="raw", bufs=4))
         psum = ctx.enter_context(tc.psum_pool(name="psum", bufs=1))
         ctx.enter_context(tc.manual_schedule())
 
@@ -47,9 +49,11 @@ def tile_ctc_prior_head_s4_kernel(
         w_p = [[keep.tile([P, 4, P, 2], U8, name=f"w_p{c}_{g}", align_bytes=64) for g in range(KG)] for c in range(NG)]
         ws_p = [[keep.tile([P, 4, P], U8, name=f"ws_p{c}_{g}", align_bytes=64) for g in range(KG)] for c in range(NG)]
         gain_c = keep.tile([P, NG, 4], BF16, name="gain_c")
-        prior_b = keep.tile([P, V], BF16, name="prior_b")
-        bias_b = keep.tile([P, V], BF16, name="bias_b")
-        log_p = keep.tile([P, V], F32, name="log_p")
+        gain_f = keep.tile([P, NG, 4], F32, name="gain_f")
+        prior_r = keep.tile([16, P], BF16, name="prior_r")
+        bias_r = keep.tile([16, P], BF16, name="bias_r")
+        log_r = keep.tile([16, P], F32, name="log_r")
+        rows = keep.tile([16, P], F32, name="rows")
         shift = keep.tile([P, V], F32, name="shift")
         warm = keep.tile([P, 2], F32, name="warm")
         h_c = [[keep.tile([P, Q], U32, name=f"h_c{c}_{q}", align_bytes=64) for q in range(4)] for c in range(NG)]
@@ -64,32 +68,8 @@ def tile_ctc_prior_head_s4_kernel(
                 in_=scales[:, 4 * quad : 4 * quad + 4, :].rearrange("g q n -> q g n").bitcast(I32),
             )
 
-        load_words(nc.sync, w_raw[0], w_words, 0)
-        load_words(nc.gpsimd, x_w[0], x_words, 0)
-        nc.vector.memset(ws_raw[:].bitcast(I32), 0)
-        nc.vector.memset(x_s[:].bitcast(I32), 0)
-        nc.vector.memset(warm[:], 1.0)
-        nc.scalar.activation(out=warm[:, 1:2], in_=warm[:, 0:1], func=LN)
-        for quad in range(4):
-            load_scale_quad(nc.sync, ws_raw, w_scales, quad)
-        for quad in range(4):
-            load_scale_quad(nc.sync if quad < 3 else nc.gpsimd, x_s, x_scales, quad)
-        nc.gpsimd.dma_start(out=gain_c[:], in_=gain.rearrange("(c p t) -> p c t", c=NG, t=4))
-        for g in (1, 2):
-            load_words(nc.sync, w_raw[g], w_words, g)
-            load_words(nc.sync, x_w[g], x_words, g)
-        nc.sync.dma_start(out=prior_b[:], in_=prior_ratio.partition_broadcast(P))
-        load_words(nc.sync, w_raw[3], w_words, 3)
-        load_words(nc.sync, x_w[3], x_words, 3)
-        nc.sync.dma_start(out=bias_b[:], in_=bias.partition_broadcast(P))
-        nc.vector.memset(u_s[:].bitcast(I32), 0)
-        for quad in range(4):
-            load_scale_quad(nc.sync, u_s, u_scales, quad)
-        for c in range(NG):
-            nc.sync.dma_start(out=u_w[c][:].bitcast(I32), in_=u_words[c].rearrange("p n t -> p (n t)").bitcast(I32))
-
-        def order_scales(c, g):
-            nc.vector.tensor_copy(
+        def order_scales(engine, c, g):
+            engine.tensor_copy(
                 out=ws_p[c][g][:],
                 in_=ws_raw[:, g, 512 * c : 512 * (c + 1)].rearrange("p (m t) -> p t m", t=4),
             )
@@ -100,15 +80,47 @@ def tile_ctc_prior_head_s4_kernel(
                 in_=w_raw[g][:, 1024 * c : 1024 * (c + 1)].rearrange("p (m t e) -> p t m e", t=4, e=2),
             )
 
-        for c, g in ((0, 0), (0, 1), (1, 0), (0, 2), (1, 1), (0, 3), (1, 2), (1, 3)):
-            order_scales(c, g)
-            order_words(c, g)
-        nc.scalar.activation(out=log_p[:], in_=prior_b[:], func=LN)
-        nc.scalar.activation(out=warm[:, 1:2], in_=warm[:, 0:1], func=TANH)
-        nc.vector.tensor_tensor(out=shift[:], in0=bias_b[:], in1=log_p[:], op=SUB)
-
         def bank_tile(i):
             return psum.tile([P, 512], F32, name=f"bank{i}", tag=f"bank{i}")
+
+        load_words(nc.sync, w_raw[0], w_words, 0)
+        load_words(nc.gpsimd, x_w[0], x_words, 0)
+        nc.vector.memset(ws_raw[:].bitcast(I32), 0)
+        nc.vector.memset(x_s[:].bitcast(I32), 0)
+        nc.vector.memset(warm[:], 1.0)
+        nc.scalar.activation(out=warm[:, 1:2], in_=warm[:, 0:1], func=LN)
+        for quad in range(4):
+            load_scale_quad(nc.sync, ws_raw, w_scales, quad)
+        for quad in range(4):
+            load_scale_quad(nc.sync if quad < 3 else nc.gpsimd, x_s, x_scales, quad)
+        nc.gpsimd.dma_start(out=prior_r[:], in_=prior_ratio.rearrange("(c p) -> c p", p=P))
+        nc.gpsimd.dma_start(out=bias_r[:], in_=bias.rearrange("(c p) -> c p", p=P))
+        nc.gpsimd.dma_start(out=gain_c[:], in_=gain.rearrange("(c p t) -> p c t", c=NG, t=4))
+        for g in range(1, KG):
+            load_words(nc.sync, w_raw[g], w_words, g)
+            load_words(nc.sync, x_w[g], x_words, g)
+        nc.vector.memset(u_s[:].bitcast(I32), 0)
+        for quad in range(4):
+            load_scale_quad(nc.sync, u_s, u_scales, quad)
+
+        nc.scalar.activation(out=log_r[:], in_=prior_r[:], func=LN)
+        nc.scalar.activation(out=warm[:, 1:2], in_=warm[:, 0:1], func=TANH)
+
+        for g in range(KG):
+            order_scales(nc.vector, 0, g)
+            order_words(0, g)
+        for g in range(KG):
+            order_scales(nc.gpsimd, 1, g)
+        for c in range(NG):
+            nc.sync.dma_start(out=u_w[c][:].bitcast(I32), in_=u_words[c].rearrange("p n t -> p (n t)").bitcast(I32))
+        order_words(1, 0)
+        nc.vector.tensor_tensor(out=rows[:], in0=bias_r[:], in1=log_r[:], op=SUB)
+        parked = out[M - 1 : M, :]
+        nc.sync.dma_start(out=parked.rearrange("o (c p) -> (o c) p", p=P), in_=rows[:])
+        nc.sync.dma_start(out=shift[:], in_=parked.rearrange("o n -> (o n)").partition_broadcast(P))
+        for g in range(1, KG):
+            order_words(1, g)
+        nc.vector.tensor_copy(out=gain_f[:], in_=gain_c[:])
 
         def project(dst, c, g, t, m0, width):
             nc.tensor.matmul_mx(
@@ -121,92 +133,129 @@ def tile_ctc_prior_head_s4_kernel(
                 stop=(g == KG - 1),
             )
 
-        def multiply(c, q, th, n0):
+        held = {}
+
+        def new_hb(c, q):
             hb = hb_pool.tile([P, Q, 4], BF16, name="hb", align_bytes=64)
+            held[(c, q)] = hb
+            return hb[:].rearrange("p (b i) t -> p b t i", i=4)
+
+        def multiply(c, q, th, n0):
             nc.vector.tensor_tensor(
-                out=hb[:].rearrange("p (b i) t -> p b t i", i=4),
+                out=new_hb(c, q),
                 in0=th[:, :, n0 : n0 + Q].rearrange("p t (b i) -> p b t i", i=4),
                 in1=gain_c[:, c, :].unsqueeze(1).unsqueeze(3).to_broadcast([P, Q // 4, 4, 4]),
                 op=MULT,
             )
-            return hb
 
-        def quantise(c, q, hb):
+        def scale(c, q, th, n0):
+            hg = hb_pool.tile([P, 4, Q], BF16, name="hg", align_bytes=64)
+            for t in range(4):
+                nc.scalar.activation(
+                    out=hg[:, t, :], in_=th[:, t, n0 : n0 + Q], func=COPY, scale=gain_f[:, c, t : t + 1]
+                )
+            return hg
+
+        def weave(c, q, hg):
+            nc.vector.tensor_copy(out=new_hb(c, q), in_=hg[:].rearrange("p t (b i) -> p b t i", i=4))
+
+        def quantise(c, q):
             nc.vector.quantize_mx(
-                out=h_c[c][q][:].bitcast(FP8X4), scales=h_s[c][q][:], in_=hb[:].rearrange("p n t -> p (n t)")
+                out=h_c[c][q][:].bitcast(FP8X4),
+                scales=h_s[c][q][:],
+                in_=held[(c, q)][:].rearrange("p n t -> p (n t)"),
             )
 
-        banks = [[bank_tile(4 * h + t) for t in range(4)] for h in range(2)]
-        for g in range(KG):
-            for h in range(2):
-                for t in range(4):
-                    project(banks[h][t][:], 0, g, t, HALF * h, HALF)
-        th0 = [keep.tile([P, 4, HALF], F32, name=f"th0_{h}") for h in range(2)]
-        for h in range(2):
+        def project_half(c, h, first, k_outer):
+            th = keep.tile([P, 4, HALF], F32, name=f"th_half{c}{h}")
+            banks = [bank_tile(first + t) for t in range(4)]
+            for a in range(KG):
+                for b in range(4):
+                    g, t = (a, b) if k_outer else (b, a)
+                    project(banks[t][:], c, g, t, HALF * h, HALF)
             for t in range(4):
-                nc.scalar.activation(out=th0[h][:, t, :], in_=banks[h][t][:], func=TANH)
+                nc.scalar.activation(out=th[:, t, :], in_=banks[t][:], func=TANH)
+            return th
 
-        def project_quarter(q):
+        def project_quarter(c, q, first):
             th = th_pool.tile([P, 4, Q], F32, name="th")
             for pair in range(2):
-                bank = bank_tile(2 * (q % 2) + pair)
+                bank = bank_tile(first + pair)
                 for j in range(2):
                     for g in range(KG):
-                        project(bank[:, Q * j : Q * (j + 1)], 1, g, 2 * pair + j, Q * q, Q)
+                        project(bank[:, Q * j : Q * (j + 1)], c, g, 2 * pair + j, Q * q, Q)
                 nc.scalar.activation(
                     out=th[:, 2 * pair : 2 * pair + 2, :].rearrange("p t n -> p (t n)"), in_=bank[:], func=TANH
                 )
             return th
 
-        def score(q, side, off):
-            step = 0
-            for m in range(2):
-                for v in range(4):
-                    bank = bank_tile(4 + step % 4 if q < 2 else (4 + step) % 8)
-                    for c in range(NG):
-                        nc.tensor.matmul_mx(
-                            out=bank[:],
-                            lhsT=h_c[c][q][:, P * m : P * (m + 1)].bitcast(FP8X4),
-                            lhsT_scale=h_s[c][q][:, P * m : P * (m + 1)],
-                            rhs=u_w[c][:, 512 * v : 512 * (v + 1)].bitcast(FP8X4),
-                            rhs_scale=u_s[:, c, 512 * v : 512 * (v + 1)],
-                            start=(c == 0),
-                            stop=(c == NG - 1),
-                        )
-                    res = res_pool.tile([P, 512], F32, name="res")
-                    if step in off:
-                        raw = res_pool.tile([P, 512], F32, name="raw")
-                        nc.scalar.copy(out=raw[:], in_=bank[:])
-                        nc.gpsimd.tensor_tensor(out=res[:], in0=raw[:], in1=shift[:, 512 * v : 512 * (v + 1)], op=ADD)
-                    else:
-                        nc.vector.tensor_tensor(out=res[:], in0=bank[:], in1=shift[:, 512 * v : 512 * (v + 1)], op=ADD)
-                    m0 = Q * q + P * m
-                    nc.sync.dma_start(out=out[m0 : m0 + P, 512 * v : 512 * (v + 1)], in_=res[:])
-                    for job in side.get(step, []):
-                        job()
-                    step += 1
+        turn = [0]
 
-        held = {}
+        def store(m0, v, width, res):
+            nc.sync.dma_start(out=out[m0 : m0 + P, 512 * v : 512 * v + width], in_=res[:])
 
-        def mul_job(c, q, th, n0):
-            held[(c, q)] = multiply(c, q, th, n0)
+        late = []
 
-        def quant_job(c, q):
-            quantise(c, q, held[(c, q)])
+        def score(q, m, ring, jobs, off, pair=2):
+            m0 = Q * q + P * m
+            for v in range(4):
+                bank = bank_tile(ring[turn[0] % len(ring)])
+                turn[0] += 1
+                for c in range(NG):
+                    nc.tensor.matmul_mx(
+                        out=bank[:],
+                        lhsT=h_c[c][q][:, P * m : P * (m + 1)].bitcast(FP8X4),
+                        lhsT_scale=h_s[c][q][:, P * m : P * (m + 1)],
+                        rhs=u_w[c][:, 512 * v : 512 * (v + 1)].bitcast(FP8X4),
+                        rhs_scale=u_s[:, c, 512 * v : 512 * (v + 1)],
+                        start=(c == 0),
+                        stop=(c == NG - 1),
+                    )
+                if v % pair == 0:
+                    res = res_pool.tile([P, 512 * pair], F32, name="res")
+                part = res[:, 512 * (v % pair) : 512 * (v % pair + 1)]
+                if v in off:
+                    raw = raw_pool.tile([P, 512], F32, name="raw")
+                    nc.scalar.copy(out=raw[:], in_=bank[:])
+                    nc.gpsimd.tensor_tensor(out=part, in0=raw[:], in1=shift[:, 512 * v : 512 * (v + 1)], op=ADD)
+                else:
+                    nc.vector.tensor_tensor(out=part, in0=bank[:], in1=shift[:, 512 * v : 512 * (v + 1)], op=ADD)
+                if v % pair == pair - 1:
+                    late.append((turn[0] + (2 if v in off else 0), m0, v - pair + 1, 512 * pair, res))
+                for item in [x for x in late if x[0] == turn[0]]:
+                    store(*item[1:])
+                for job in jobs.get(v, []):
+                    job()
 
-        mul_job(0, 0, th0[0], 0)
-        mul_job(0, 1, th0[0], Q)
-        quant_job(0, 0)
-        th_q0 = project_quarter(0)
-        th_q1 = project_quarter(1)
-        mul_job(1, 0, th_q0, 0)
-        quant_job(0, 1)
-        quant_job(1, 0)
-        mul_job(0, 2, th0[1], 0)
-        score(0, {1: [lambda: mul_job(1, 1, th_q1, 0)], 2: [lambda: quant_job(0, 2)], 3: [lambda: quant_job(1, 1)]}, (1, 3, 5))
-        th_q2 = project_quarter(2)
-        mul_job(0, 3, th0[1], Q)
-        score(1, {1: [lambda: mul_job(1, 2, th_q2, 0)], 2: [lambda: quant_job(0, 3)], 3: [lambda: quant_job(1, 2)]}, (1, 3, 5))
-        th_q3 = project_quarter(3)
-        score(2, {1: [lambda: mul_job(1, 3, th_q3, 0)], 3: [lambda: quant_job(1, 3)]}, (1, 3, 5))
-        score(3, {}, (0, 2, 4, 6))
+        th_00 = project_half(0, 0, 0, True)
+        th_20 = project_quarter(0, 2, 4)
+        multiply(0, 0, th_00, 0)
+        hg_01 = scale(0, 1, th_00, Q)
+        quantise(0, 0)
+        weave(0, 1, hg_01)
+        th_10 = project_half(1, 0, 0, False)
+        hg_20 = scale(0, 2, th_20, 0)
+        quantise(0, 1)
+        th_30 = project_quarter(0, 3, 6)
+        multiply(1, 0, th_10, 0)
+        hg_11 = scale(1, 1, th_10, Q)
+        quantise(1, 0)
+        weave(0, 2, hg_20)
+        ring = (4, 5, 6, 7)
+        score(0, 0, ring, {1: [lambda: weave(1, 1, hg_11)], 3: [lambda: quantise(0, 2)]}, ())
+        hg_30 = scale(0, 3, th_30, 0)
+        score(0, 1, ring, {0: [lambda: quantise(1, 1)], 2: [lambda: weave(0, 3, hg_30)]}, ())
+        th_21 = project_quarter(1, 2, 0)
+        hg_21 = scale(1, 2, th_21, 0)
+        score(1, 0, ring, {0: [lambda: quantise(0, 3)], 3: [lambda: weave(1, 2, hg_21)]}, ())
+        score(1, 1, ring, {1: [lambda: quantise(1, 2)]}, ())
+        th_31 = project_quarter(1, 3, 2)
+        hg_31 = scale(1, 3, th_31, 0)
+        ring = (4, 5, 6, 7, 0, 1)
+        score(2, 0, ring, {2: [lambda: weave(1, 3, hg_31)]}, ())
+        score(2, 1, ring, {0: [lambda: quantise(1, 3)]}, (3,))
+        ring = (4, 5, 6, 7, 0, 1, 2, 3)
+        score(3, 0, ring, {}, (1, 3))
+        score(3, 1, ring, {}, (0,), 1)
+        for item in [x for x in late if x[0] > turn[0]]:
+            store(*item[1:])

@@ -40,10 +40,10 @@ def tile_ctc_prior_head_s4_kernel(
         psum = ctx.enter_context(tc.psum_pool(name="psum", bufs=1))
         ctx.enter_context(tc.manual_schedule())
 
-        x_w = [keep.tile([P, 2 * M], U8, name=f"x_w{g}", align_bytes=64) for g in range(KG)]
-        w_raw = [keep.tile([P, 2 * N], U8, name=f"w_raw{g}", align_bytes=64) for g in range(KG)]
-        x_s = keep.tile([P, KG, M], U8, name="x_s", align_bytes=64)
-        ws_raw = keep.tile([P, KG, N], U8, name="ws_raw", align_bytes=64)
+        x_w = [keep.tile([P, KG, M], U8, name=f"x_w{h}", align_bytes=64) for h in range(2)]
+        w_raw = keep.tile([P, KG, 2 * N], U8, name="w_raw", align_bytes=64)
+        x_s = [keep.tile([P, KG, HALF], U8, name=f"x_s{i}", align_bytes=64) for i in range(2)]
+        ws_raw = [keep.tile([P, KG, 512], U8, name=f"ws_raw{i}", align_bytes=64) for i in range(2)]
         u_s = keep.tile([P, NG, V], U8, name="u_s", align_bytes=64)
         u_w = [keep.tile([P, V], U32, name=f"u_w{g}", align_bytes=64) for g in range(NG)]
         w_p = [[keep.tile([P, 4, P, 2], U8, name=f"w_p{c}_{g}", align_bytes=64) for g in range(KG)] for c in range(NG)]
@@ -59,8 +59,17 @@ def tile_ctc_prior_head_s4_kernel(
         h_c = [[keep.tile([P, Q], U32, name=f"h_c{c}_{q}", align_bytes=64) for q in range(4)] for c in range(NG)]
         h_s = [[keep.tile([P, Q], U8, name=f"h_s{c}_{q}", align_bytes=64) for q in range(4)] for c in range(NG)]
 
-        def load_words(engine, tile, words, g):
-            engine.dma_start(out=tile[:].bitcast(I32), in_=words[g].bitcast(I32))
+        def load_w(g0, g1):
+            nc.sync.dma_start(
+                out=w_raw[:, g0:g1, :].bitcast(I32),
+                in_=w_words[g0:g1].bitcast(I32).rearrange("g p n -> p g n"),
+            )
+
+        def load_x(engine, h, g0, g1):
+            engine.dma_start(
+                out=x_w[h][:, g0:g1, :].bitcast(I32),
+                in_=x_words[g0:g1, :, M * h : M * (h + 1)].bitcast(I32).rearrange("g p n -> p g n"),
+            )
 
         def load_scale_quad(engine, tile, scales, quad):
             engine.dma_start(
@@ -68,57 +77,66 @@ def tile_ctc_prior_head_s4_kernel(
                 in_=scales[:, 4 * quad : 4 * quad + 4, :].rearrange("g q n -> q g n").bitcast(I32),
             )
 
-        def order_scales(engine, c, g):
-            engine.tensor_copy(
+        def bank_tile(i):
+            return psum.tile([P, 512], F32, name=f"bank{i}", tag=f"bank{i}")
+
+        def order_scales(c, g):
+            nc.vector.tensor_copy(
                 out=ws_p[c][g][:],
-                in_=ws_raw[:, g, 512 * c : 512 * (c + 1)].rearrange("p (m t) -> p t m", t=4),
+                in_=ws_raw[c][:, g, :].rearrange("p (m t) -> p t m", t=4),
             )
 
         def order_words(c, g):
             nc.vector.tensor_copy(
                 out=w_p[c][g][:],
-                in_=w_raw[g][:, 1024 * c : 1024 * (c + 1)].rearrange("p (m t e) -> p t m e", t=4, e=2),
+                in_=w_raw[:, g, 1024 * c : 1024 * (c + 1)].rearrange("p (m t e) -> p t m e", t=4, e=2),
             )
 
-        def bank_tile(i):
-            return psum.tile([P, 512], F32, name=f"bank{i}", tag=f"bank{i}")
-
-        load_words(nc.sync, w_raw[0], w_words, 0)
-        load_words(nc.gpsimd, x_w[0], x_words, 0)
-        nc.vector.memset(ws_raw[:].bitcast(I32), 0)
-        nc.vector.memset(x_s[:].bitcast(I32), 0)
-        nc.vector.memset(warm[:], 1.0)
+        nc.gpsimd.memset(warm[:], 1.0)
         nc.scalar.activation(out=warm[:, 1:2], in_=warm[:, 0:1], func=LN)
-        for quad in range(4):
-            load_scale_quad(nc.sync, ws_raw, w_scales, quad)
-        for quad in range(4):
-            load_scale_quad(nc.sync if quad < 3 else nc.gpsimd, x_s, x_scales, quad)
+        load_w(0, 1)
+        load_x(nc.sync, 0, 0, 1)
         nc.gpsimd.dma_start(out=prior_r[:], in_=prior_ratio.rearrange("(c p) -> c p", p=P))
         nc.gpsimd.dma_start(out=bias_r[:], in_=bias.rearrange("(c p) -> c p", p=P))
-        nc.gpsimd.dma_start(out=gain_c[:], in_=gain.rearrange("(c p t) -> p c t", c=NG, t=4))
-        for g in range(1, KG):
-            load_words(nc.sync, w_raw[g], w_words, g)
-            load_words(nc.sync, x_w[g], x_words, g)
+        for half in range(2):
+            nc.vector.memset(ws_raw[half][:].bitcast(I32), 0)
+            nc.vector.memset(x_s[half][:].bitcast(I32), 0)
         nc.vector.memset(u_s[:].bitcast(I32), 0)
+        for quad in range(4):
+            load_scale_quad(nc.sync, ws_raw[0], w_scales[:, :, 0:512], quad)
+        for quad in range(4):
+            load_scale_quad(nc.sync, x_s[0], x_scales[:, :, 0:HALF], quad)
+        load_w(1, 2)
+        load_x(nc.sync, 0, 1, 2)
+        load_w(2, 4)
+        load_x(nc.sync, 0, 2, 4)
+        for quad in range(4):
+            load_scale_quad(nc.sync, ws_raw[1], w_scales[:, :, 512:N], quad)
+        load_x(nc.sync, 1, 0, 4)
+        for quad in range(4):
+            load_scale_quad(nc.sync if quad < 2 else nc.gpsimd, x_s[1], x_scales[:, :, HALF:M], quad)
+        nc.gpsimd.dma_start(out=gain_c[:], in_=gain.rearrange("(c p t) -> p c t", c=NG, t=4))
         for quad in range(4):
             load_scale_quad(nc.sync, u_s, u_scales, quad)
 
         nc.scalar.activation(out=log_r[:], in_=prior_r[:], func=LN)
         nc.scalar.activation(out=warm[:, 1:2], in_=warm[:, 0:1], func=TANH)
-
         for g in range(KG):
-            order_scales(nc.vector, 0, g)
+            order_scales(0, g)
             order_words(0, g)
-        for g in range(KG):
-            order_scales(nc.gpsimd, 1, g)
-        for c in range(NG):
-            nc.sync.dma_start(out=u_w[c][:].bitcast(I32), in_=u_words[c].rearrange("p n t -> p (n t)").bitcast(I32))
-        order_words(1, 0)
-        nc.vector.tensor_tensor(out=rows[:], in0=bias_r[:], in1=log_r[:], op=SUB)
+            if g == 0:
+                nc.vector.tensor_tensor(out=rows[:], in0=bias_r[:], in1=log_r[:], op=SUB)
         parked = out[M - 1 : M, :]
         nc.sync.dma_start(out=parked.rearrange("o (c p) -> (o c) p", p=P), in_=rows[:])
-        nc.sync.dma_start(out=shift[:], in_=parked.rearrange("o n -> (o n)").partition_broadcast(P))
-        for g in range(1, KG):
+        for c in range(NG):
+            nc.sync.dma_start(out=u_w[c][:].bitcast(I32), in_=u_words[c].rearrange("p n t -> p (n t)").bitcast(I32))
+        for h in range(2):
+            nc.sync.dma_start(
+                out=shift[:, 1024 * h : 1024 * (h + 1)],
+                in_=parked[:, 1024 * h : 1024 * (h + 1)].rearrange("o n -> (o n)").partition_broadcast(P),
+            )
+        for g in range(KG):
+            order_scales(1, g)
             order_words(1, g)
         nc.vector.tensor_copy(out=gain_f[:], in_=gain_c[:])
 
@@ -127,8 +145,8 @@ def tile_ctc_prior_head_s4_kernel(
                 out=dst,
                 lhsT=w_p[c][g][:, t].rearrange("p m e -> p (m e)").bitcast(FP4X4),
                 lhsT_scale=ws_p[c][g][:, t],
-                rhs=x_w[g][:, 2 * m0 : 2 * (m0 + width)].bitcast(FP4X4),
-                rhs_scale=x_s[:, g, m0 : m0 + width],
+                rhs=x_w[m0 // HALF][:, g, 2 * (m0 % HALF) : 2 * (m0 % HALF + width)].bitcast(FP4X4),
+                rhs_scale=x_s[m0 // HALF][:, g, m0 % HALF : m0 % HALF + width],
                 start=(g == 0),
                 stop=(g == KG - 1),
             )
@@ -221,12 +239,23 @@ def tile_ctc_prior_head_s4_kernel(
                 else:
                     nc.vector.tensor_tensor(out=part, in0=bank[:], in1=shift[:, 512 * v : 512 * (v + 1)], op=ADD)
                 if v % pair == pair - 1:
-                    late.append((turn[0] + (2 if v in off else 0), m0, v - pair + 1, 512 * pair, res))
+                    late.append((turn[0] + (2 if v in off else 1 if pair == 2 and v - 1 in off else 0), m0, v - pair + 1, 512 * pair, res))
                 for item in [x for x in late if x[0] == turn[0]]:
                     store(*item[1:])
                 for job in jobs.get(v, []):
                     job()
 
+        idle = bank_tile(7)
+        for i in range(2):
+            nc.tensor.matmul_mx(
+                out=idle[:],
+                lhsT=w_raw[:, 0, 0:256].bitcast(FP4X4),
+                lhsT_scale=ws_raw[0][:, 0, 0:P],
+                rhs=w_raw[:, 0, 0:1024].bitcast(FP4X4),
+                rhs_scale=ws_raw[0][:, 0, :],
+                start=True,
+                stop=True,
+            )
         th_00 = project_half(0, 0, 0, True)
         th_20 = project_quarter(0, 2, 4)
         multiply(0, 0, th_00, 0)
@@ -253,9 +282,9 @@ def tile_ctc_prior_head_s4_kernel(
         hg_31 = scale(1, 3, th_31, 0)
         ring = (4, 5, 6, 7, 0, 1)
         score(2, 0, ring, {2: [lambda: weave(1, 3, hg_31)]}, ())
-        score(2, 1, ring, {0: [lambda: quantise(1, 3)]}, (3,))
+        score(2, 1, ring, {0: [lambda: quantise(1, 3)]}, (0,))
         ring = (4, 5, 6, 7, 0, 1, 2, 3)
-        score(3, 0, ring, {}, (1, 3))
+        score(3, 0, ring, {}, (0, 2))
         score(3, 1, ring, {}, (0,), 1)
         for item in [x for x in late if x[0] > turn[0]]:
             store(*item[1:])

from contextlib import ExitStack

import concourse.mybir as mybir

M, K, N, V = 1024, 2048, 1024, 2048
FLOPS = 2 * M * K * N + 2 * M * N * V
BYTES = 2 * (K * M // 2 + K // 32 * M) + N * V + N // 32 * V + 2 * N + 4 * V + 4 * M * V

F32 = mybir.dt.float32
BF16 = mybir.dt.bfloat16
I32 = mybir.dt.int32
U32 = mybir.dt.uint32
U8 = mybir.dt.uint8
FP4X4 = mybir.dt.float4_e2m1fn_x4
FP8X4 = mybir.dt.float8_e4m3fn_x4
ADD = mybir.AluOpType.add
SUB = mybir.AluOpType.subtract
MULT = mybir.AluOpType.mult
COPY = mybir.ActivationFunctionType.Copy
LN = mybir.ActivationFunctionType.Ln
TANH = mybir.ActivationFunctionType.Tanh

P = 128
KG = K // 512
NG = N // 512
HALF = 512
Q = 256


def tile_ctc_prior_head_s4_kernel(
    tc, x_words, x_scales, w_words, w_scales, gain, u_words, u_scales, bias, prior_ratio, out
):
    nc = tc.nc
    with ExitStack() as ctx:
        keep = ctx.enter_context(tc.tile_pool(name="keep", bufs=1))
        th_pool = ctx.enter_context(tc.tile_pool(name="th", bufs=3))
        hb_pool = ctx.enter_context(tc.tile_pool(name="hb", bufs=4))
        res_pool = ctx.enter_context(tc.tile_pool(name="res", bufs=10))
        raw_pool = ctx.enter_context(tc.tile_pool(name="raw", bufs=4))
        psum = ctx.enter_context(tc.psum_pool(name="psum", bufs=1))
        ctx.enter_context(tc.manual_schedule())

        x_w = [keep.tile([P, KG, M], U8, name=f"x_w{h}", align_bytes=64) for h in range(2)]
        w_raw = keep.tile([P, KG, 2 * N], U8, name="w_raw", align_bytes=64)
        x_s = [keep.tile([P, KG, HALF], U8, name=f"x_s{i}", align_bytes=64) for i in range(2)]
        ws_raw = [keep.tile([P, KG, 512], U8, name=f"ws_raw{i}", align_bytes=64) for i in range(2)]
        u_s = keep.tile([P, NG, V], U8, name="u_s", align_bytes=64)
        u_w = [keep.tile([P, V], U32, name=f"u_w{g}", align_bytes=64) for g in range(NG)]
        w_p = [[keep.tile([P, 4, P, 2], U8, name=f"w_p{c}_{g}", align_bytes=64) for g in range(KG)] for c in range(NG)]
        ws_p = [[keep.tile([P, 4, P], U8, name=f"ws_p{c}_{g}", align_bytes=64) for g in range(KG)] for c in range(NG)]
        gain_c = keep.tile([P, NG, 4], BF16, name="gain_c")
        gain_f = keep.tile([P, NG, 4], F32, name="gain_f")
        prior_r = keep.tile([16, P], BF16, name="prior_r")
        bias_r = keep.tile([16, P], BF16, name="bias_r")
        log_r = keep.tile([16, P], F32, name="log_r")
        rows = keep.tile([16, P], F32, name="rows")
        shift = keep.tile([P, V], F32, name="shift")
        warm = keep.tile([P, 2], F32, name="warm")
        h_c = [[keep.tile([P, Q], U32, name=f"h_c{c}_{q}", align_bytes=64) for q in range(4)] for c in range(NG)]
        h_s = [[keep.tile([P, Q], U8, name=f"h_s{c}_{q}", align_bytes=64) for q in range(4)] for c in range(NG)]

        def load_w(g0, g1):
            nc.sync.dma_start(
                out=w_raw[:, g0:g1, :].bitcast(I32),
                in_=w_words[g0:g1].bitcast(I32).rearrange("g p n -> p g n"),
            )

        def load_x(engine, h, g0, g1):
            engine.dma_start(
                out=x_w[h][:, g0:g1, :].bitcast(I32),
                in_=x_words[g0:g1, :, M * h : M * (h + 1)].bitcast(I32).rearrange("g p n -> p g n"),
            )

        def load_scale_quad(engine, tile, scales, quad):
            engine.dma_start(
                out=tile[32 * quad : 32 * quad + 4].bitcast(I32),
                in_=scales[:, 4 * quad : 4 * quad + 4, :].rearrange("g q n -> q g n").bitcast(I32),
            )

        def bank_tile(i):
            return psum.tile([P, 512], F32, name=f"bank{i}", tag=f"bank{i}")

        def order_scales(c, g):
            nc.vector.tensor_copy(
                out=ws_p[c][g][:],
                in_=ws_raw[c][:, g, :].rearrange("p (m t) -> p t m", t=4),
            )

        def order_words(c, g):
            nc.vector.tensor_copy(
                out=w_p[c][g][:],
                in_=w_raw[:, g, 1024 * c : 1024 * (c + 1)].rearrange("p (m t e) -> p t m e", t=4, e=2),
            )

        nc.gpsimd.memset(warm[:], 1.0)
        nc.scalar.activation(out=warm[:, 1:2], in_=warm[:, 0:1], func=LN)
        load_w(0, 1)
        load_x(nc.sync, 0, 0, 1)
        nc.gpsimd.dma_start(out=prior_r[:], in_=prior_ratio.rearrange("(c p) -> c p", p=P))
        nc.gpsimd.dma_start(out=bias_r[:], in_=bias.rearrange("(c p) -> c p", p=P))
        for half in range(2):
            nc.vector.memset(ws_raw[half][:].bitcast(I32), 0)
            nc.vector.memset(x_s[half][:].bitcast(I32), 0)
        nc.vector.memset(u_s[:].bitcast(I32), 0)
        for quad in range(4):
            load_scale_quad(nc.sync, ws_raw[0], w_scales[:, :, 0:512], quad)
        for quad in range(4):
            load_scale_quad(nc.sync, x_s[0], x_scales[:, :, 0:HALF], quad)
        load_w(1, 2)
        load_x(nc.sync, 0, 1, 2)
        load_w(2, 4)
        load_x(nc.sync, 0, 2, 4)
        for quad in range(4):
            load_scale_quad(nc.sync, ws_raw[1], w_scales[:, :, 512:N], quad)
        load_x(nc.sync, 1, 0, 4)
        for quad in range(4):
            load_scale_quad(nc.sync if quad < 2 else nc.gpsimd, x_s[1], x_scales[:, :, HALF:M], quad)
        nc.gpsimd.dma_start(out=gain_c[:], in_=gain.rearrange("(c p t) -> p c t", c=NG, t=4))
        for quad in range(4):
            load_scale_quad(nc.sync, u_s, u_scales, quad)

        nc.scalar.activation(out=log_r[:], in_=prior_r[:], func=LN)
        nc.scalar.activation(out=warm[:, 1:2], in_=warm[:, 0:1], func=TANH)
        for g in range(KG):
            order_scales(0, g)
            order_words(0, g)
            if g == 0:
                nc.vector.tensor_tensor(out=rows[:], in0=bias_r[:], in1=log_r[:], op=SUB)
        parked = out[M - 1 : M, :]
        nc.sync.dma_start(out=parked.rearrange("o (c p) -> (o c) p", p=P), in_=rows[:])
        for c in range(NG):
            nc.sync.dma_start(out=u_w[c][:].bitcast(I32), in_=u_words[c].rearrange("p n t -> p (n t)").bitcast(I32))
        for h in range(2):
            nc.sync.dma_start(
                out=shift[:, 1024 * h : 1024 * (h + 1)],
                in_=parked[:, 1024 * h : 1024 * (h + 1)].rearrange("o n -> (o n)").partition_broadcast(P),
            )
        for g in range(KG):
            order_scales(1, g)
            order_words(1, g)
        nc.vector.tensor_copy(out=gain_f[:], in_=gain_c[:])

        def project(dst, c, g, t, m0, width):
            nc.tensor.matmul_mx(
                out=dst,
                lhsT=w_p[c][g][:, t].rearrange("p m e -> p (m e)").bitcast(FP4X4),
                lhsT_scale=ws_p[c][g][:, t],
                rhs=x_w[m0 // HALF][:, g, 2 * (m0 % HALF) : 2 * (m0 % HALF + width)].bitcast(FP4X4),
                rhs_scale=x_s[m0 // HALF][:, g, m0 % HALF : m0 % HALF + width],
                start=(g == 0),
                stop=(g == KG - 1),
            )

        held = {}

        def new_hb(c, q):
            hb = hb_pool.tile([P, Q, 4], BF16, name="hb", align_bytes=64)
            held[(c, q)] = hb
            return hb[:].rearrange("p (b i) t -> p b t i", i=4)

        def multiply(c, q, th, n0):
            nc.vector.tensor_tensor(
                out=new_hb(c, q),
                in0=th[:, :, n0 : n0 + Q].rearrange("p t (b i) -> p b t i", i=4),
                in1=gain_c[:, c, :].unsqueeze(1).unsqueeze(3).to_broadcast([P, Q // 4, 4, 4]),
                op=MULT,
            )

        def scale(c, q, th, n0):
            hg = hb_pool.tile([P, 4, Q], BF16, name="hg", align_bytes=64)
            for t in range(4):
                nc.scalar.activation(
                    out=hg[:, t, :], in_=th[:, t, n0 : n0 + Q], func=COPY, scale=gain_f[:, c, t : t + 1]
                )
            return hg

        def weave(c, q, hg):
            nc.vector.tensor_copy(out=new_hb(c, q), in_=hg[:].rearrange("p t (b i) -> p b t i", i=4))

        def quantise(c, q):
            nc.vector.quantize_mx(
                out=h_c[c][q][:].bitcast(FP8X4),
                scales=h_s[c][q][:],
                in_=held[(c, q)][:].rearrange("p n t -> p (n t)"),
            )

        def project_half(c, h, first, k_outer):
            th = keep.tile([P, 4, HALF], F32, name=f"th_half{c}{h}")
            banks = [bank_tile(first + t) for t in range(4)]
            for a in range(KG):
                for b in range(4):
                    g, t = (a, b) if k_outer else (b, a)
                    project(banks[t][:], c, g, t, HALF * h, HALF)
            for t in range(4):
                nc.scalar.activation(out=th[:, t, :], in_=banks[t][:], func=TANH)
            return th

        def project_quarter(c, q, first):
            th = th_pool.tile([P, 4, Q], F32, name="th")
            for pair in range(2):
                bank = bank_tile(first + pair)
                for j in range(2):
                    for g in range(KG):
                        project(bank[:, Q * j : Q * (j + 1)], c, g, 2 * pair + j, Q * q, Q)
                nc.scalar.activation(
                    out=th[:, 2 * pair : 2 * pair + 2, :].rearrange("p t n -> p (t n)"), in_=bank[:], func=TANH
                )
            return th

        turn = [0]

        def store(m0, v, width, res):
            nc.sync.dma_start(out=out[m0 : m0 + P, 512 * v : 512 * v + width], in_=res[:])

        late = []

        def score(q, m, ring, jobs, off, pair=2):
            m0 = Q * q + P * m
            for v in range(4):
                bank = bank_tile(ring[turn[0] % len(ring)])
                turn[0] += 1
                for c in range(NG):
                    nc.tensor.matmul_mx(
                        out=bank[:],
                        lhsT=h_c[c][q][:, P * m : P * (m + 1)].bitcast(FP8X4),
                        lhsT_scale=h_s[c][q][:, P * m : P * (m + 1)],
                        rhs=u_w[c][:, 512 * v : 512 * (v + 1)].bitcast(FP8X4),
                        rhs_scale=u_s[:, c, 512 * v : 512 * (v + 1)],
                        start=(c == 0),
                        stop=(c == NG - 1),
                    )
                if v % pair == 0:
                    res = res_pool.tile([P, 512 * pair], F32, name="res")
                part = res[:, 512 * (v % pair) : 512 * (v % pair + 1)]
                if v in off:
                    raw = raw_pool.tile([P, 512], F32, name="raw")
                    nc.scalar.copy(out=raw[:], in_=bank[:])
                    nc.gpsimd.tensor_tensor(out=part, in0=raw[:], in1=shift[:, 512 * v : 512 * (v + 1)], op=ADD)
                else:
                    nc.vector.tensor_tensor(out=part, in0=bank[:], in1=shift[:, 512 * v : 512 * (v + 1)], op=ADD)
                if v % pair == pair - 1:
                    late.append((turn[0] + (2 if v in off else 1 if pair == 2 and v - 1 in off else 0), m0, v - pair + 1, 512 * pair, res))
                for item in [x for x in late if x[0] == turn[0]]:
                    store(*item[1:])
                for job in jobs.get(v, []):
                    job()

        idle = bank_tile(7)
        for i in range(2):
            nc.tensor.matmul_mx(
                out=idle[:],
                lhsT=w_raw[:, 0, 0:256].bitcast(FP4X4),
                lhsT_scale=ws_raw[0][:, 0, 0:P],
                rhs=w_raw[:, 0, 0:1024].bitcast(FP4X4),
                rhs_scale=ws_raw[0][:, 0, :],
                start=True,
                stop=True,
            )
        th_00 = project_half(0, 0, 0, True)
        th_20 = project_quarter(0, 2, 4)
        multiply(0, 0, th_00, 0)
        hg_01 = scale(0, 1, th_00, Q)
        quantise(0, 0)
        weave(0, 1, hg_01)
        th_10 = project_half(1, 0, 0, False)
        hg_20 = scale(0, 2, th_20, 0)
        quantise(0, 1)
        th_30 = project_quarter(0, 3, 6)
        multiply(1, 0, th_10, 0)
        hg_11 = scale(1, 1, th_10, Q)
        quantise(1, 0)
        weave(0, 2, hg_20)
        ring = (4, 5, 6, 7)
        score(0, 0, ring, {1: [lambda: weave(1, 1, hg_11)], 3: [lambda: quantise(0, 2)]}, ())
        hg_30 = scale(0, 3, th_30, 0)
        score(0, 1, ring, {0: [lambda: quantise(1, 1)], 2: [lambda: weave(0, 3, hg_30)]}, ())
        th_21 = project_quarter(1, 2, 0)
        hg_21 = scale(1, 2, th_21, 0)
        score(1, 0, ring, {0: [lambda: quantise(0, 3)], 3: [lambda: weave(1, 2, hg_21)]}, ())
        score(1, 1, ring, {1: [lambda: quantise(1, 2)]}, ())
        th_31 = project_quarter(1, 3, 2)
        hg_31 = scale(1, 3, th_31, 0)
        ring = (4, 5, 6, 7, 0, 1)
        score(2, 0, ring, {2: [lambda: weave(1, 3, hg_31)]}, ())
        score(2, 1, ring, {0: [lambda: quantise(1, 3)]}, (0,))
        ring = (4, 5, 6, 7, 0, 1, 2, 3)
        score(3, 0, ring, {}, (0, 2))
        score(3, 1, ring, {}, (0,), 1)
        for item in [x for x in late if x[0] > turn[0]]:
            store(*item[1:])
